import numpy as np
CORES = [2,18,34,50,66,82,98,114]
N = 8
ROOT = 3
def setup_inputs(rng):
    return {"x": rng.standard_normal((N, 128, 512), dtype=np.float32)}
def reference(x):
    y = np.full((N, 128, N * 512), np.nan, x.dtype)
    y[ROOT] = np.concatenate(list(x), axis=1)
    return {"y": y}

@@ -1,0 +1,108 @@
+K = 4
+UR = 128 // K
+UW = 512 // K
+G = 2
+LAT = 3.0
+
+ASSIGN = {0: "AAAA", 1: "AAAA", 2: "BBAA", 4: "BBBB", 5: "CCCB", 6: "CCCC", 7: "DDDD"}
+
+SCRATCH = {
+    "d": ("dram", [8 * K, 128, UW], "float32"),
+}
+SEMAPHORES = ["l0", "l1", "l2", "l3", "sent", "stored"] + ["a%d" % i for i in range(32)]
+
+
+def plan(cores, root_rank):
+    root = cores[root_rank]
+    rchip = root // 8
+    mate = rchip ^ 1
+    streams = {}
+    for p in "ABCD":
+        lists = [[(j, q) for q in range(K) if ASSIGN[j][q] == p] for j in sorted(ASSIGN)]
+        lists = [x for x in lists if x]
+        lists.sort(key=lambda x: (x[0][1], -len(x)))
+        out = []
+        i = 0
+        while any(i < len(x) for x in lists):
+            out += [x[i] for x in lists if i < len(x)]
+            i += 1
+        streams[p] = out
+    hops = {}
+    est = {}
+    for p in "ABCD":
+        for pos, (j, q) in enumerate(streams[p]):
+            src = cores[j]
+            base = (src // 8) * 8
+            alt = pos % 2
+            if p == "A":
+                h = [src, root]
+            elif p == "B":
+                h = [src, base + 4 + alt, root]
+            elif p == "C":
+                h = [src, mate * 8 + 2 + alt, root]
+            else:
+                h = [src, base + 6 + alt, mate * 8 + 6 + alt, root]
+            hops[(j, q)] = h
+            est[(j, q)] = LAT * (len(h) - 1) + pos + 1
+    groups = []
+    for j in sorted(ASSIGN):
+        q = 0
+        while q < K:
+            n = 1
+            while n < G and q + n < K and ASSIGN[j][q + n] == ASSIGN[j][q]:
+                n += 1
+            groups.append((max(est[(j, q + i)] for i in range(n)), j, q, n))
+            q += n
+    groups.sort()
+    return hops, est, groups
+
+
+def rank_program(g, core, T, topo):
+    s = T.sem
+    arr = [s.a0, s.a1, s.a2, s.a3, s.a4, s.a5, s.a6, s.a7, s.a8, s.a9, s.a10, s.a11, s.a12, s.a13, s.a14, s.a15,
+           s.a16, s.a17, s.a18, s.a19, s.a20, s.a21, s.a22, s.a23, s.a24, s.a25, s.a26, s.a27, s.a28, s.a29,
+           s.a30, s.a31]
+    lds = [s.l0, s.l1, s.l2, s.l3]
+    cores = list(T.cores)
+    root_rank = T.root if T.root is not None else 3
+    root = cores[root_rank]
+    hops, est, groups = plan(cores, root_rank)
+    rank = T.rank_of(core)
+
+    def engines(a, b):
+        m = topo.mask(a, b)
+        return m, bin(m).count("1")
+
+    if core == root:
+        g.dma_start(T.y[:, 512 * root_rank:512 * (root_rank + 1)], T.x[:, :]).then_inc(s.stored, 16)
+        n = 1
+        for e, j, q, cnt in groups:
+            for i in range(cnt):
+                h = hops[(j, q + i)]
+                g.wait_ge(arr[j * K + q + i], engines(h[-2], root)[1])
+            g.dma_start(T.y[q * UR:(q + cnt) * UR, 512 * j:512 * (j + 1)],
+                        T.d[j * K + q:j * K + q + cnt]).then_inc(s.stored, 16)
+            n += 1
+        g.wait_ge(s.stored, 16 * n)
+        return
+
+    work = sorted((est[u] - LAT * (len(h) - 1 - h.index(core)), u, h.index(core))
+                  for u, h in hops.items() if core in h[:-1])
+    if not work:
+        return
+    if rank is not None:
+        work.sort(key=lambda w: w[1][1])
+        for t, (j, q), k in work:
+            g.dma_start(T.d[j * K + q], T.x[q * UR:(q + 1) * UR, :]).then_inc(lds[q], 16)
+    sent = 0
+    for t, (j, q), k in work:
+        h = hops[(j, q)]
+        if k == 0:
+            g.wait_ge(lds[q], 16)
+        else:
+            g.wait_ge(arr[j * K + q], engines(h[k - 1], core)[1])
+        m, ne = engines(core, h[k + 1])
+        rid, pid, se = topo.addr(h[k + 1])
+        g.remote_dma(T.d[j * K + q], T.d[j * K + q], arr[j * K + q], s.sent, pid, rid, m)
+        sent += ne
+    g.wait_ge(s.sent, sent)

@@ -4,7 +4,7 @@ UW = 512 // K
 G = 2
 LAT = 3.0
 
-ASSIGN = {0: "AAAA", 1: "AAAA", 2: "BBAA", 4: "BBBB", 5: "CCCB", 6: "CCCC", 7: "DDDD"}
+ASSIGN = {0: "AAAA", 1: "AAAA", 2: "BBBB", 4: "CBBB", 5: "CCCC", 6: "DDCC", 7: "DDDD"}
 
 SCRATCH = {
     "d": ("dram", [8 * K, 128, UW], "float32"),

@@ -1,7 +1,7 @@
 K = 4
 UR = 128 // K
 UW = 512 // K
-G = 2
+G = 4
 LAT = 3.0
 
 ASSIGN = {0: "AAAA", 1: "AAAA", 2: "BBBB", 4: "CBBB", 5: "CCCC", 6: "DDCC", 7: "DDDD"}

@@ -1,36 +1,31 @@
 K = 4
-UR = 128 // K
 UW = 512 // K
-G = 4
 LAT = 3.0
 
 ASSIGN = {0: "AAAA", 1: "AAAA", 2: "BBBB", 4: "CBBB", 5: "CCCC", 6: "DDCC", 7: "DDDD"}
+COPIES = [(0, 1), (2, 2), (4, 5), (6, 7)]
 
 SCRATCH = {
-    "d": ("dram", [8 * K, 128, UW], "float32"),
+    "land": ("sbuf", [128, 4096], "float32"),
 }
-SEMAPHORES = ["l0", "l1", "l2", "l3", "sent", "stored"] + ["a%d" % i for i in range(32)]
+SEMAPHORES = ["ld", "sent", "stored"] + ["a%d" % i for i in range(32)]
 
 
 def plan(cores, root_rank):
     root = cores[root_rank]
-    rchip = root // 8
-    mate = rchip ^ 1
-    streams = {}
+    mate = (root // 8) ^ 1
+    hops = {}
+    est = {}
     for p in "ABCD":
         lists = [[(j, q) for q in range(K) if ASSIGN[j][q] == p] for j in sorted(ASSIGN)]
         lists = [x for x in lists if x]
         lists.sort(key=lambda x: (x[0][1], -len(x)))
-        out = []
+        stream = []
         i = 0
         while any(i < len(x) for x in lists):
-            out += [x[i] for x in lists if i < len(x)]
+            stream += [x[i] for x in lists if i < len(x)]
             i += 1
-        streams[p] = out
-    hops = {}
-    est = {}
-    for p in "ABCD":
-        for pos, (j, q) in enumerate(streams[p]):
+        for pos, (j, q) in enumerate(stream):
             src = cores[j]
             base = (src // 8) * 8
             alt = pos % 2
@@ -44,17 +39,7 @@ def plan(cores, root_rank):
                 h = [src, base + 6 + alt, mate * 8 + 6 + alt, root]
             hops[(j, q)] = h
             est[(j, q)] = LAT * (len(h) - 1) + pos + 1
-    groups = []
-    for j in sorted(ASSIGN):
-        q = 0
-        while q < K:
-            n = 1
-            while n < G and q + n < K and ASSIGN[j][q + n] == ASSIGN[j][q]:
-                n += 1
-            groups.append((max(est[(j, q + i)] for i in range(n)), j, q, n))
-            q += n
-    groups.sort()
-    return hops, est, groups
+    return hops, est
 
 
 def rank_program(g, core, T, topo):
@@ -62,11 +47,10 @@ def rank_program(g, core, T, topo):
     arr = [s.a0, s.a1, s.a2, s.a3, s.a4, s.a5, s.a6, s.a7, s.a8, s.a9, s.a10, s.a11, s.a12, s.a13, s.a14, s.a15,
            s.a16, s.a17, s.a18, s.a19, s.a20, s.a21, s.a22, s.a23, s.a24, s.a25, s.a26, s.a27, s.a28, s.a29,
            s.a30, s.a31]
-    lds = [s.l0, s.l1, s.l2, s.l3]
     cores = list(T.cores)
     root_rank = T.root if T.root is not None else 3
     root = cores[root_rank]
-    hops, est, groups = plan(cores, root_rank)
+    hops, est = plan(cores, root_rank)
     rank = T.rank_of(core)
 
     def engines(a, b):
@@ -76,12 +60,11 @@ def rank_program(g, core, T, topo):
     if core == root:
         g.dma_start(T.y[:, 512 * root_rank:512 * (root_rank + 1)], T.x[:, :]).then_inc(s.stored, 16)
         n = 1
-        for e, j, q, cnt in groups:
-            for i in range(cnt):
-                h = hops[(j, q + i)]
-                g.wait_ge(arr[j * K + q + i], engines(h[-2], root)[1])
-            g.dma_start(T.y[q * UR:(q + cnt) * UR, 512 * j:512 * (j + 1)],
-                        T.d[j * K + q:j * K + q + cnt]).then_inc(s.stored, 16)
+        for j0, j1 in COPIES:
+            for j in range(j0, j1 + 1):
+                for q in range(K):
+                    g.wait_ge(arr[j * K + q], engines(hops[(j, q)][-2], root)[1])
+            g.dma_start(T.y[:, 512 * j0:512 * (j1 + 1)], T.land[:, 512 * j0:512 * (j1 + 1)]).then_inc(s.stored, 16)
             n += 1
         g.wait_ge(s.stored, 16 * n)
         return
@@ -92,17 +75,16 @@ def rank_program(g, core, T, topo):
         return
     if rank is not None:
         work.sort(key=lambda w: w[1][1])
-        for t, (j, q), k in work:
-            g.dma_start(T.d[j * K + q], T.x[q * UR:(q + 1) * UR, :]).then_inc(lds[q], 16)
+        g.dma_start(T.land[:, 512 * rank:512 * (rank + 1)], T.x[:, :]).then_inc(s.ld, 16)
+        g.wait_ge(s.ld, 16)
     sent = 0
     for t, (j, q), k in work:
         h = hops[(j, q)]
-        if k == 0:
-            g.wait_ge(lds[q], 16)
-        else:
+        if k > 0:
             g.wait_ge(arr[j * K + q], engines(h[k - 1], core)[1])
         m, ne = engines(core, h[k + 1])
         rid, pid, se = topo.addr(h[k + 1])
-        g.remote_dma(T.d[j * K + q], T.d[j * K + q], arr[j * K + q], s.sent, pid, rid, m)
+        ap = T.land[:, 512 * j + UW * q:512 * j + UW * (q + 1)]
+        g.remote_dma(ap, ap, arr[j * K + q], s.sent, pid, rid, m)
         sent += ne
     g.wait_ge(s.sent, sent)

K = 4
UW = 512 // K
LAT = 3.0

ASSIGN = {0: "AAAA", 1: "AAAA", 2: "BBBB", 4: "CBBB", 5: "CCCC", 6: "DDCC", 7: "DDDD"}
COPIES = [(0, 1), (2, 2), (4, 5), (6, 7)]

SCRATCH = {
    "land": ("sbuf", [128, 4096], "float32"),
}
SEMAPHORES = ["ld", "sent", "stored"] + ["a%d" % i for i in range(32)]


def plan(cores, root_rank):
    root = cores[root_rank]
    mate = (root // 8) ^ 1
    hops = {}
    est = {}
    for p in "ABCD":
        lists = [[(j, q) for q in range(K) if ASSIGN[j][q] == p] for j in sorted(ASSIGN)]
        lists = [x for x in lists if x]
        lists.sort(key=lambda x: (x[0][1], -len(x)))
        stream = []
        i = 0
        while any(i < len(x) for x in lists):
            stream += [x[i] for x in lists if i < len(x)]
            i += 1
        for pos, (j, q) in enumerate(stream):
            src = cores[j]
            base = (src // 8) * 8
            alt = pos % 2
            if p == "A":
                h = [src, root]
            elif p == "B":
                h = [src, base + 4 + alt, root]
            elif p == "C":
                h = [src, mate * 8 + 2 + alt, root]
            else:
                h = [src, base + 6 + alt, mate * 8 + 6 + alt, root]
            hops[(j, q)] = h
            est[(j, q)] = LAT * (len(h) - 1) + pos + 1
    return hops, est


def rank_program(g, core, T, topo):
    s = T.sem
    arr = [s.a0, s.a1, s.a2, s.a3, s.a4, s.a5, s.a6, s.a7, s.a8, s.a9, s.a10, s.a11, s.a12, s.a13, s.a14, s.a15,
           s.a16, s.a17, s.a18, s.a19, s.a20, s.a21, s.a22, s.a23, s.a24, s.a25, s.a26, s.a27, s.a28, s.a29,
           s.a30, s.a31]
    cores = list(T.cores)
    root_rank = T.root if T.root is not None else 3
    root = cores[root_rank]
    hops, est = plan(cores, root_rank)
    rank = T.rank_of(core)

    def engines(a, b):
        m = topo.mask(a, b)
        return m, bin(m).count("1")

    if core == root:
        g.dma_start(T.y[:, 512 * root_rank:512 * (root_rank + 1)], T.x[:, :]).then_inc(s.stored, 16)
        n = 1
        for j0, j1 in COPIES:
            for j in range(j0, j1 + 1):
                for q in range(K):
                    g.wait_ge(arr[j * K + q], engines(hops[(j, q)][-2], root)[1])
            g.dma_start(T.y[:, 512 * j0:512 * (j1 + 1)], T.land[:, 512 * j0:512 * (j1 + 1)]).then_inc(s.stored, 16)
            n += 1
        g.wait_ge(s.stored, 16 * n)
        return

    work = sorted((est[u] - LAT * (len(h) - 1 - h.index(core)), u, h.index(core))
                  for u, h in hops.items() if core in h[:-1])
    if not work:
        return
    if rank is not None:
        work.sort(key=lambda w: w[1][1])
        g.dma_start(T.land[:, 512 * rank:512 * (rank + 1)], T.x[:, :]).then_inc(s.ld, 16)
        g.wait_ge(s.ld, 16)
    sent = 0
    for t, (j, q), k in work:
        h = hops[(j, q)]
        if k > 0:
            g.wait_ge(arr[j * K + q], engines(h[k - 1], core)[1])
        m, ne = engines(core, h[k + 1])
        rid, pid, se = topo.addr(h[k + 1])
        ap = T.land[:, 512 * j + UW * q:512 * j + UW * (q + 1)]
        g.remote_dma(ap, ap, arr[j * K + q], s.sent, pid, rid, m)
        sent += ne
    g.wait_ge(s.sent, sent)
